import numpy as np
import ml_dtypes


def mxq(x, axis, fmt="e4m3"):
    dtype, down = {"e4m3": (ml_dtypes.float8_e4m3fn, 7), "e5m2": (ml_dtypes.float8_e5m2, 14)}[fmt]
    v = np.moveaxis(np.asarray(x, np.float32).astype(ml_dtypes.bfloat16).astype(np.float64), axis, -1)
    blocks = v.reshape(v.shape[:-1] + (-1, 32))
    amax = np.abs(blocks).max(-1, keepdims=True)
    byte = np.maximum(np.where(amax > 0, np.frexp(amax)[1] - 1 + 127, 0) - down, 1)
    scale = np.exp2(byte - 127.0)
    codes = (blocks / scale).astype(np.float32).astype(dtype).astype(np.float64)
    return np.moveaxis((codes * scale).reshape(v.shape), -1, axis)


WIDE = False


def mx_kscale(k):
    if not WIDE:
        return np.ones(k)
    levels = np.array([10, -10, 5, -5, 0])
    if k % 512:
        return np.exp2(np.random.permutation(np.resize(levels, k // 32))).repeat(32)
    a = np.empty((k // 512, 16))
    for p in range(k // 512):
        a[p, :8] = np.random.permutation(np.resize(levels, 8))
        for g in range(8):
            far = levels[np.abs(levels - a[p, g]) >= 10]
            a[p, g + 8] = far[np.random.randint(len(far))]
    return np.exp2(a.ravel()).repeat(32)


BF16 = ml_dtypes.bfloat16


def bf(x):
    return np.asarray(x, np.float32).astype(BF16)


def f64(x):
    return np.asarray(x).astype(np.float64)


N, D, F = 1024, 1024, 1024

EPS_RESIDUAL = 0.3


def draw0():
    s = mx_kscale(D)
    t = mx_kscale(N)
    return {
        "x": bf(np.random.standard_normal((N, D)) * s[None, :]),
        "w": bf(np.random.standard_normal((D, F)) / np.sqrt(D) / s[:, None]),
        "adj": bf(np.random.standard_normal((N, N)) / np.sqrt(N) * t[None, :]),
        "a1": bf(np.random.standard_normal(F) / np.sqrt(F)),
        "a2": bf(np.random.standard_normal(F) / np.sqrt(F)),
        "ri": bf((1.0 + 0.1 * np.random.standard_normal(N)) / t),
        "ro": bf(1.0 + 0.1 * np.random.standard_normal(N)),
    }


def signed_gate(z, a1, a2):
    s = np.sum(z * a1[None, :], axis=-1)
    t = np.sum(z * a2[None, :], axis=-1)
    return np.tanh(s[:, None] + t[None, :])


def core(x, w, adj, a1, a2, ri, ro):
    z = mxq(f64(x), 1, "e4m3") @ mxq(f64(w), 0, "e4m3")
    c = f64(adj) * signed_gate(z, f64(a1), f64(a2))
    zs = z * f64(ri)[:, None]
    m = mxq(c, 1, "e4m3") @ mxq(zs, 0, "e4m3")
    return EPS_RESIDUAL * z + f64(ro)[:, None] * m


def e4m3fn_bytes(y):
    return np.clip(np.asarray(y, np.float64), -448.0, 448.0).astype(np.float32).astype(ml_dtypes.float8_e4m3fn).view(np.uint8)


def e4m3fn_values(b):
    return np.asarray(b, np.uint8).view(ml_dtypes.float8_e4m3fn).astype(np.float64)


def setup_inputs():
    d = draw0()
    x0 = np.asarray(d['x']).astype(np.float64)
    s = (np.max(np.abs(x0), axis=(0,), keepdims=True) / 448.0).astype(np.float32)
    out = {}
    for k, v in d.items():
        if k == 'x':
            out['x_bytes'] = e4m3fn_bytes(x0 / s.astype(np.float64))
            out['x_scale'] = s
        else:
            out[k] = v
    return out


def reference(x_bytes, x_scale, w, adj, a1, a2, ri, ro):
    return core(e4m3fn_values(x_bytes) * x_scale.astype(np.float64), w, adj, a1, a2, ri, ro)

@@ -1,0 +1,344 @@
+from contextlib import ExitStack
+
+import concourse.mybir as mybir
+from concourse.masks import make_identity
+
+F32 = mybir.dt.float32
+BF16 = mybir.dt.bfloat16
+U32 = mybir.dt.uint32
+U8 = mybir.dt.uint8
+FP8 = mybir.dt.float8_e4m3fn
+FP8X4 = mybir.dt.float8_e4m3fn_x4
+MULT = mybir.AluOpType.mult
+ADD = mybir.AluOpType.add
+ACT = mybir.ActivationFunctionType
+
+NODES, FEATS = 1024, 1024
+P = 128
+FLOPS = 2 * 2 * NODES * FEATS * 1024
+ORDER = """
+    xc00v xc02s xc03v xt00 xm00 xc01s wm001g xt02 xm02 xt03 wm000g xc10s xm03 xt01 wm011g wm010s xm01
+    xc13s wq01 wq00 xc11s xq01 ac xq00 xc12s xt11 aco wm111g zt03 xm11 wm110s xt10 wm101g xt12 xm10
+    zto03s z020 wm100s zt02 xm12 z030 zto02s xt13 wq10 zo020s zt01 wq11 zo030s z000 xm13 zto01s z010
+    zo000s zt00 zo010s xq11 z011 zto00s xq10 z031 zs0111 zm000 z001 zo031s z021 zs0110 sm0 zm003
+    zs0011 zo011s zs0311 zo001s zo021s zm002 zs0310 zs0010 zt11 zs0210 zt12 zm011 z131 zs0211 zto12s
+    zto11s zs1311 zm013 zt13 z121 zs1310 zto13s z101 zs1210 zm012 zo131s ss0 zt10 zo121s zs1010 z111
+    zto10s zm010 zs1011 sp0 zo111s zs1211 sm1 zo101s zs1110 zm001 th000 zs1111 zm111 th010 at01 ss1
+    z120 zq00 z110 zo120s cm011 zm112 sp1 th100 at10 cm010 at00 zq01 th110 z130 cm101 zm110 z100
+    zo110v cm100 zo100s zm113 zo130s at11 th030 cm111 zm103 cm001 th020 cq01 cm000 zm101 th120 cm110
+    at02 at12 zq11 th130 cq10 cq00 cm121 zm102 m01 cm021 fs01 cm020 zm100 cm120 at03 at13 cq11 zq10
+    m11 cq02 m21 fs11 cm031 m30 fs21 cq12 m10 cm131 fg21 m00 f30 m20 f10 fg11 m40 f00 m50 f20 fg01
+    m31 cm130 m41 fs31 cm030 f50 fg31 f40 cq13 m51 f41 cq03 f51 m61 m70 f61 m71 f70 m60 f71 f60
+"""
+NB = 4
+
+
+def tile_fagcnsignedtanhpropagation_kernel(
+    tc, x_bytes, x_scale, w, adj, a1, a2, ri, ro, out
+):
+    nc = tc.nc
+    with ExitStack() as ctx:
+        keep = ctx.enter_context(tc.tile_pool(name="keep", bufs=1))
+        stage = ctx.enter_context(tc.tile_pool(name="stage", bufs=2))
+        psum = ctx.enter_context(tc.psum_pool(name="psum", bufs=1))
+        ctx.enter_context(tc.manual_schedule())
+
+        xs_col = keep.tile([P, 2, 4], F32, name="xs_col")
+        a_bc = keep.tile([P, 2, 1024], BF16, name="a_bc")
+        ri_raw = keep.tile([P, 2, 4], BF16, name="ri_raw")
+        ro_raw = keep.tile([P, 2, 4], BF16, name="ro_raw")
+        ri_col = keep.tile([P, 8], F32, name="ri_col")
+        ro_col = keep.tile([P, 8], F32, name="ro_col")
+        ident = keep.tile([P, P], F32, name="ident")
+        ident_bf = keep.tile([P, P], BF16, name="ident_bf")
+        a_col = keep.tile([P, NB, 2], F32, name="a_col")
+        warm = keep.tile([P, 1], F32, name="warm")
+        x_in = [keep.tile([P, 4, 1024], U8, name="x_in%d" % g) for g in range(2)]
+        w_in = [[keep.tile([P, 4, 512], BF16, name="w_in%d%d" % (h, k)) for k in range(2)] for h in range(2)]
+        adj_in = [keep.tile([P, 4, 1024], BF16, name="adj_in%d" % g) for g in range(2)]
+        x_grp = [keep.tile([P, 2, 512, 4], BF16, name="x_grp%d" % g, align_bytes=64) for g in range(2)]
+        x_codes = [keep.tile([P, 2, 512], U32, name="x_codes%d" % g, align_bytes=64) for g in range(2)]
+        x_sc = [keep.tile([P, 2, 512], U8, name="x_sc%d" % g, align_bytes=64) for g in range(2)]
+        w_codes = [[keep.tile([P, 512], U32, name="w_codes%d%d" % (h, k), align_bytes=64) for k in range(2)] for h in range(2)]
+        w_sc = [[keep.tile([P, 512], U8, name="w_sc%d%d" % (h, k), align_bytes=64) for k in range(2)] for h in range(2)]
+        z03 = [[keep.tile([P, 4, 512], F32, name="z03_%d%d" % (g, h)) for h in range(2)] for g in range(2)]
+        zs_codes = [[keep.tile([P, 512], U32, name="zs_codes%d%d" % (g, h), align_bytes=64) for h in range(2)] for g in range(2)]
+        zs_sc = [[keep.tile([P, 512], U8, name="zs_sc%d%d" % (g, h), align_bytes=64) for h in range(2)] for g in range(2)]
+        c_codes = [[keep.tile([P, 256], U32, name="c_codes%d%d" % (j, u), align_bytes=64) for u in range(4)] for j in range(2)]
+        c_sc = [[keep.tile([P, 256], U8, name="c_sc%d%d" % (j, u), align_bytes=64) for u in range(4)] for j in range(2)]
+        part = [keep.tile([P, 2, 4], F32, name="part%d" % g) for g in range(2)]
+        score = [keep.tile([P, 2, 4], F32, name="score%d" % g) for g in range(2)]
+
+        x_view = x_bytes.rearrange("(g p t) k -> g p t k", p=P, t=4)
+        w_view = w.rearrange("(k p j) f -> k p j f", p=P, j=4)
+        adj_view = adj.rearrange("(g p t) j -> g p t j", p=P, t=4)
+        out_view = out.rearrange("(g p t) f -> g t p f", p=P, t=4)
+        nc.scalar.dma_start(out=xs_col[:], in_=x_scale.rearrange("o (k p t) -> p (o k) t", p=P, t=4))
+        nc.scalar.dma_start(out=ri_raw[:], in_=ri.rearrange("(g p t) -> p g t", p=P, t=4))
+        nc.scalar.dma_start(out=ro_raw[:], in_=ro.rearrange("(g p t) -> p g t", p=P, t=4))
+        for g in range(2):
+            for t in (0, 2):
+                nc.sync.dma_start(out=x_in[g][:, t : t + 2, :], in_=x_view[g][:, t : t + 2, :])
+            for k in range(2):
+                nc.sync.dma_start(out=w_in[g][k][:], in_=w_view[k][:, :, 512 * g : 512 * g + 512])
+        nc.sync.dma_start(out=a_bc[:, 0, :], in_=a1.partition_broadcast(P))
+        nc.sync.dma_start(out=a_bc[:, 1, :], in_=a2.partition_broadcast(P))
+        for g in range(2):
+            for t in (0, 2):
+                nc.sync.dma_start(out=adj_in[g][:, t : t + 2, :], in_=adj_view[g][:, t : t + 2, :])
+
+        nc.vector.memset(warm[:], 0.0)
+        nc.scalar.activation(out=warm[:], in_=warm[:], func=ACT.Tanh)
+        make_identity(nc, ident[:])
+        make_identity(nc, ident_bf[:])
+
+        x_wide = {}
+        x_ps = {}
+
+        def x_widen(g, t, eng):
+            x_row = stage.tile([P, 1024], BF16, name="x_row", bufs=6)
+            if eng == "v":
+                nc.vector.tensor_copy(out=x_row[:], in_=x_in[g][:, t, :].bitcast(FP8))
+            else:
+                nc.scalar.copy(out=x_row[:], in_=x_in[g][:, t, :].bitcast(FP8))
+            x_wide[g, t] = x_row
+
+        def x_turn(g, t):
+            ps = psum.tile([P, 2, 2, P], F32, name="turn", bufs=2)
+            words = x_wide[g, t][:].bitcast(F32)
+            for k in range(2):
+                for u in range(2):
+                    nc.tensor.transpose(ps[:, k, u, :], words[:, 256 * k + u : 256 * (k + 1) : 2], ident[:])
+            x_ps[g, t] = ps
+
+        def x_scale_out(g, t):
+            flat = x_ps[g, t][:].rearrange("p k u r -> p (k u r)").bitcast(BF16)
+            for k in range(2):
+                nc.vector.tensor_tensor(
+                    out=x_grp[g][:, k, P * t : P * t + P, :].rearrange("p r (u e) -> p r u e", u=2),
+                    in0=flat[:, 512 * k : 512 * k + 512].rearrange("p (u r e) -> p r u e", u=2, e=2),
+                    in1=xs_col[:, k, :].unsqueeze(1).to_broadcast([P, P, 4]).rearrange("p r (u e) -> p r u e", u=2),
+                    op=MULT,
+                )
+
+        def x_quant(g, k):
+            nc.vector.quantize_mx(
+                out=x_codes[g][:, k, :].bitcast(FP8X4), scales=x_sc[g][:, k, :],
+                in_=x_grp[g][:, k, :, :].rearrange("p n j -> p (n j)"),
+            )
+
+        w_grp = {}
+
+        def w_mix(h, k, half, eng):
+            if (h, k) not in w_grp:
+                grp = stage.tile([P, 512, 4], BF16, name="grp", bufs=4, align_bytes=64)
+                w_grp[h, k] = grp
+            lo = 256 * half
+            dst = w_grp[h, k][:, lo : lo + 256, :]
+            src = w_in[h][k][:, :, lo : lo + 256].rearrange("p j f -> p f j")
+            if eng == "v":
+                nc.vector.tensor_copy(out=dst, in_=src)
+            elif eng == "s":
+                nc.scalar.copy(out=dst, in_=src)
+            else:
+                nc.gpsimd.tensor_scalar(out=dst, in0=src, scalar1=1.0, scalar2=0.0, op0=MULT, op1=ADD)
+
+        def w_quant(h, k):
+            nc.vector.quantize_mx(
+                out=w_codes[h][k][:].bitcast(FP8X4), scales=w_sc[h][k][:],
+                in_=w_grp[h, k][:].rearrange("p n j -> p (n j)"),
+            )
+
+        zt_sb = {}
+        acc_ps = {}
+
+        def zt_mm(g, b):
+            h, c = divmod(b, 4)
+            ps = psum.tile([P, 512], F32, name="acc", bufs=4)
+            for k in range(2):
+                nc.tensor.matmul_mx(
+                    out=ps[:],
+                    lhsT=w_codes[h][k][:, P * c : P * c + P].bitcast(FP8X4), lhsT_scale=w_sc[h][k][:, P * c : P * c + P],
+                    rhs=x_codes[g][:, k, :].bitcast(FP8X4), rhs_scale=x_sc[g][:, k, :],
+                    start=(k == 0), stop=(k == 1),
+                )
+            acc_ps["zt", g, b] = ps
+
+        def a_cols():
+            ps = psum.tile([P, NB, 2, P], BF16, name="turn", bufs=2)
+            for b in range(NB):
+                for a in range(2):
+                    nc.tensor.transpose(ps[:, b, a, :], a_bc[:, a, P * b : P * b + P], ident_bf[:])
+            acc_ps["a"] = ps
+
+        def a_cols_out():
+            nc.vector.tensor_copy(out=a_col[:], in_=acc_ps["a"][:, :, :, 0])
+            nc.vector.tensor_scalar(out=ri_col[:], in0=ri_raw[:].rearrange("p g t -> p (g t)"), scalar1=1.0 / 0.3, scalar2=None, op0=MULT)
+            nc.vector.tensor_copy(out=ro_col[:], in_=ro_raw[:].rearrange("p g t -> p (g t)"))
+
+        def zt_out(g, b, eng):
+            sb = stage.tile([P, 512], F32, name="zt_sb%d" % b, bufs=1)
+            if eng == "v":
+                nc.vector.tensor_copy(out=sb[:], in_=acc_ps["zt", g, b][:])
+            else:
+                nc.scalar.copy(out=sb[:], in_=acc_ps["zt", g, b][:])
+            zt_sb[g, b] = sb
+
+        st_ps = {}
+
+        def score_mm(g):
+            ps = psum.tile([P, 4, 2], F32, name="turn", bufs=2)
+            for t in range(4):
+                for b in range(NB):
+                    nc.tensor.matmul(
+                        out=ps[:, t, :], lhsT=zt_sb[g, b][:, P * t : P * t + P], rhs=a_col[:, b, :],
+                        start=(b == 0), stop=(b == NB - 1),
+                    )
+            st_ps[g] = ps
+
+        def z_mm(g, t, h):
+            ps = psum.tile([P, 512], F32, name="acc", bufs=4)
+            for k in range(2):
+                nc.tensor.matmul_mx(
+                    out=ps[:],
+                    lhsT=x_codes[g][:, k, P * t : P * t + P].bitcast(FP8X4), lhsT_scale=x_sc[g][:, k, P * t : P * t + P],
+                    rhs=w_codes[h][k][:].bitcast(FP8X4), rhs_scale=w_sc[h][k][:],
+                    start=(k == 0), stop=(k == 1),
+                )
+            acc_ps["z", g, t, h] = ps
+
+        def z_out(g, t, h, eng):
+            if eng == "v":
+                nc.vector.tensor_scalar(out=z03[g][h][:, t, :], in0=acc_ps["z", g, t, h][:], scalar1=0.3, scalar2=None, op0=MULT)
+            else:
+                nc.scalar.activation(out=z03[g][h][:, t, :], in_=acc_ps["z", g, t, h][:], func=ACT.Copy, scale=0.3)
+
+        def z_score(g, t, h, a):
+            junk = stage.tile([P, 512], BF16, name="junk", bufs=2)
+            nc.vector.scalar_tensor_tensor(
+                out=junk[:], in0=acc_ps["z", g, t, h][:], scalar=1.0, in1=a_bc[:, a, 512 * h : 512 * h + 512],
+                op0=MULT, op1=MULT, accum_out=part[g][:, a, t : t + 1],
+            )
+
+        def score_sum(g):
+            nc.vector.tensor_tensor(out=score[g][:], in0=st_ps[g][:].rearrange("p t a -> p a t"), in1=part[g][:], op=ADD)
+
+        s_row = {}
+
+        def s_spread(g):
+            ps = psum.tile([P, 512], F32, name="srow%d" % g, bufs=1)
+            for t in range(4):
+                nc.tensor.transpose(ps[:, P * t : P * t + P], score[g][:, 0, t : t + 1].to_broadcast([P, P]), ident[:])
+            s_row[g] = ps
+
+        gate = {}
+
+        def gate_tanh(j, v):
+            tile = stage.tile([P, 4, 2 * P], F32, name="gate", bufs=6)
+            g, lo = v // 2, 2 * P * (v % 2)
+            for t in range(4):
+                nc.scalar.activation(out=tile[:, t, :], in_=s_row[g][:, lo : lo + 2 * P], func=ACT.Tanh, bias=score[j][:, 1, t : t + 1])
+            gate[j, v] = tile
+
+        zs_grp = {}
+
+        def zs_mul(g, h, c):
+            if (g, h) not in zs_grp:
+                grp = stage.tile([P, 512, 4], BF16, name="grp", bufs=4, align_bytes=64)
+                zs_grp[g, h] = grp
+            lo = P * c
+            nc.gpsimd.tensor_tensor(
+                out=zs_grp[g, h][:, lo : lo + P, :], in0=z03[g][h][:, :, lo : lo + P].rearrange("p t f -> p f t"),
+                in1=ri_col[:, 4 * g : 4 * g + 4].unsqueeze(1).to_broadcast([P, P, 4]), op=MULT,
+            )
+
+        def zs_quant(g, h):
+            nc.vector.quantize_mx(
+                out=zs_codes[g][h][:].bitcast(FP8X4), scales=zs_sc[g][h][:],
+                in_=zs_grp[g, h][:].rearrange("p n j -> p (n j)"),
+            )
+
+        adj_ps = {}
+        c_grp = {}
+
+        def adj_turn(j, v):
+            ps = psum.tile([P, 2, 2, P], F32, name="turn", bufs=2)
+            for i in range(2):
+                g, t = divmod(2 * v + i, 4)
+                words = adj_in[g][:, t, :].bitcast(F32)
+                for u in range(2):
+                    nc.tensor.transpose(ps[:, i, u, :], words[:, 256 * j + u : 256 * (j + 1) : 2], ident[:])
+            adj_ps[j, v] = ps
+
+        def c_mul(j, v, i):
+            if (j, v) not in c_grp:
+                grp = stage.tile([P, 2, P, 4], BF16, name="c_grp", bufs=6, align_bytes=64)
+                c_grp[j, v] = grp
+            flat = adj_ps[j, v][:].rearrange("p i u r -> p (i u r)").bitcast(BF16)
+            nc.vector.tensor_tensor(
+                out=c_grp[j, v][:, i, :, :].rearrange("p r (u e) -> p r u e", u=2),
+                in0=flat[:, 512 * i : 512 * i + 512].rearrange("p (u r e) -> p r u e", u=2, e=2),
+                in1=gate[j, v][:, :, P * i : P * i + P].rearrange("p (u e) r -> p r u e", u=2),
+                op=MULT,
+            )
+
+        def c_quant(j, v):
+            nc.vector.quantize_mx(
+                out=c_codes[j][v][:].bitcast(FP8X4), scales=c_sc[j][v][:],
+                in_=c_grp[j, v][:].rearrange("p i r j -> p (i r j)"),
+            )
+
+        def m_mm(n, h):
+            v, i = divmod(n, 2)
+            ps = psum.tile([P, 512], F32, name="acc", bufs=4)
+            for j in range(2):
+                nc.tensor.matmul_mx(
+                    out=ps[:],
+                    lhsT=c_codes[j][v][:, P * i : P * i + P].bitcast(FP8X4), lhsT_scale=c_sc[j][v][:, P * i : P * i + P],
+                    rhs=zs_codes[j][h][:].bitcast(FP8X4), rhs_scale=zs_sc[j][h][:],
+                    start=(j == 0), stop=(j == 1),
+                )
+            acc_ps["m", n, h] = ps
+
+        def store(n, h, res):
+            g, t = divmod(n, 4)
+            nc.sync.dma_start(out=out_view[g][t][:, 512 * h : 512 * h + 512], in_=res[:])
+
+        def finish(n, h):
+            g, t = divmod(n, 4)
+            res = stage.tile([P, 512], F32, name="res", bufs=4)
+            nc.vector.scalar_tensor_tensor(
+                out=res[:], in0=acc_ps["m", n, h][:], scalar=ro_col[:, n : n + 1], in1=z03[g][h][:, t, :], op0=MULT, op1=ADD,
+            )
+            store(n, h, res)
+
+        m_scaled = {}
+
+        def m_out(n, h):
+            mro = stage.tile([P, 512], F32, name="mro", bufs=3)
+            nc.scalar.activation(out=mro[:], in_=acc_ps["m", n, h][:], func=ACT.Copy, scale=ro_col[:, n : n + 1])
+            m_scaled[n, h] = mro
+
+        def finish_add(n, h):
+            g, t = divmod(n, 4)
+            res = stage.tile([P, 512], F32, name="res_g", bufs=2)
+            nc.gpsimd.tensor_tensor(out=res[:], in0=m_scaled[n, h][:], in1=z03[g][h][:, t, :], op=ADD)
+            store(n, h, res)
+
+        steps = {
+            "xc": x_widen, "xt": x_turn, "xm": x_scale_out, "xq": x_quant, "wm": w_mix, "wq": w_quant,
+            "ac": a_cols, "ao": a_cols_out, "zt": zt_mm, "zo": z_out, "zs": z_score, "sm": score_mm, "ss": score_sum, "sp": s_spread,
+            "th": gate_tanh, "zm": zs_mul, "zq": zs_quant, "at": adj_turn, "cm": c_mul, "cq": c_quant,
+            "f": finish, "fs": m_out, "fg": finish_add, "m": m_mm, "z": z_mm, "zto": zt_out,
+        }
+        for token in ORDER.split():
+            word = token.replace("aco", "ao")
+            name = "".join([ch for ch in word if ch not in "0123456789"])
+            args = [int(ch) for ch in word if ch in "0123456789"]
+            eng = []
+            if name not in steps:
+                eng = [name[-1:]]
+                name = name[:-1]
+            if name == "th":
+                args = args[:2]
+            steps[name](*args, *eng)

@@ -11,24 +11,27 @@ FP8 = mybir.dt.float8_e4m3fn
 FP8X4 = mybir.dt.float8_e4m3fn_x4
 MULT = mybir.AluOpType.mult
 ADD = mybir.AluOpType.add
+SUB = mybir.AluOpType.subtract
 ACT = mybir.ActivationFunctionType
 
 NODES, FEATS = 1024, 1024
 P = 128
 FLOPS = 2 * 2 * NODES * FEATS * 1024
 ORDER = """
-    xc00v xc02s xc03v xt00 xm00 xc01s wm001g xt02 xm02 xt03 wm000g xc10s xm03 xt01 wm011g wm010s xm01
-    xc13s wq01 wq00 xc11s xq01 ac xq00 xc12s xt11 aco wm111g zt03 xm11 wm110s xt10 wm101g xt12 xm10
-    zto03s z020 wm100s zt02 xm12 z030 zto02s xt13 wq10 zo020s zt01 wq11 zo030s z000 xm13 zto01s z010
-    zo000s zt00 zo010s xq11 z011 zto00s xq10 z031 zs0111 zm000 z001 zo031s z021 zs0110 sm0 zm003
-    zs0011 zo011s zs0311 zo001s zo021s zm002 zs0310 zs0010 zt11 zs0210 zt12 zm011 z131 zs0211 zto12s
-    zto11s zs1311 zm013 zt13 z121 zs1310 zto13s z101 zs1210 zm012 zo131s ss0 zt10 zo121s zs1010 z111
-    zto10s zm010 zs1011 sp0 zo111s zs1211 sm1 zo101s zs1110 zm001 th000 zs1111 zm111 th010 at01 ss1
-    z120 zq00 z110 zo120s cm011 zm112 sp1 th100 at10 cm010 at00 zq01 th110 z130 cm101 zm110 z100
-    zo110v cm100 zo100s zm113 zo130s at11 th030 cm111 zm103 cm001 th020 cq01 cm000 zm101 th120 cm110
-    at02 at12 zq11 th130 cq10 cq00 cm121 zm102 m01 cm021 fs01 cm020 zm100 cm120 at03 at13 cq11 zq10
-    m11 cq02 m21 fs11 cm031 m30 fs21 cq12 m10 cm131 fg21 m00 f30 m20 f10 fg11 m40 f00 m50 f20 fg01
-    m31 cm130 m41 fs31 cm030 f50 fg31 f40 cq13 m51 f41 cq03 f51 m61 m70 f61 m71 f70 m60 f71 f60
+    xc00v xc01s xc02v xc03v xt001 wm001s wm000g xt011 xm001 wm010s wm011g xm011 xt000 xc12s xq01
+    xt010 xc10s wq00 xm000 wm111g xc11s xm010 xc13s xt101 wq01 wm101s xt100 xq00 xm101 wm100s zt03
+    xm100 wm110s la xt110 zt02 wq10 zto03s zt00 xm110 zto02s ac hi03s wq11 zto00s xt111 xq10 hi02s
+    zt01 lo03g xm111 z011 zto01s zo011s xq11 hi00s lo02g zs0110 zt13 hi01s aco zt11 zs0111 lo00g z001
+    zto13v zto11s z021 zs0011 hi13s zt12 hi11g zo001s zs0211 z031 lo01g zo021s zs0010 zo031s zs0210
+    zt10 lo13g zto12s zs0310 z111 zr001s zs0311 z101 zr021s hi12g zs1111 z121 zr031s lo11g zs1010
+    zto10s zs1211 zr011s z131 zs1110 zo101s zm012g sm0 zo121s zs1311 lo12g zo111s zs1011 zo131s
+    zs1210 tz01 zm013g hi10s tz02 ss0 zs1310 zr111s sp0 lo10g zm001 tz10 zr131s tz11 zm002 th00 at00
+    zm010g zm100 sm1 zm101 zm011g zp01s cm00 zp02s tz13 zr121s tz12 zq01 zr101s at01 cq00 th01 ss1
+    zm111g zm103 at10 zm102 zm110g sp1 th10 cm01 zm113g th02 cm10 zm112g at02 zp10s zq10 at12 zp11s
+    cq10 zq11 th12 cq01 m11 cm02 th11 cm12 at11 zp13s tz00 zp12s cq02 m01 cq12 fs11 cm11 tz03 zp00s
+    fg11 at03 th03 zm000 at13 zm003 m41 fs01 cq11 zq00 zp03s m21 cm03 fg01 fs41 m30 fs21 m10 f30 fg41
+    th13 m20 f10 m31 f20 m51 fg21 fs31 cm13 m40 fs51 m00 cq03 m50 cq13 f40 fg51 m71 f00 m61 f50 fg31
+    m60 f61 m70 f71 f60 f70
 """
 NB = 4
 
@@ -48,15 +51,17 @@ def tile_fagcnsignedtanhpropagation_kernel(
         ri_raw = keep.tile([P, 2, 4], BF16, name="ri_raw")
         ro_raw = keep.tile([P, 2, 4], BF16, name="ro_raw")
         ri_col = keep.tile([P, 8], F32, name="ri_col")
+        ri_10_3 = keep.tile([P, 8], F32, name="ri_10_3")
         ro_col = keep.tile([P, 8], F32, name="ro_col")
         ident = keep.tile([P, P], F32, name="ident")
         ident_bf = keep.tile([P, P], BF16, name="ident_bf")
-        a_col = keep.tile([P, NB, 2], F32, name="a_col")
+        a_col = keep.tile([P, NB, 2], BF16, name="a_col")
         warm = keep.tile([P, 1], F32, name="warm")
         x_in = [keep.tile([P, 4, 1024], U8, name="x_in%d" % g) for g in range(2)]
-        w_in = [[keep.tile([P, 4, 512], BF16, name="w_in%d%d" % (h, k)) for k in range(2)] for h in range(2)]
-        adj_in = [keep.tile([P, 4, 1024], BF16, name="adj_in%d" % g) for g in range(2)]
-        x_grp = [keep.tile([P, 2, 512, 4], BF16, name="x_grp%d" % g, align_bytes=64) for g in range(2)]
+        x_grp = []
+        for g in range(2):
+            big = stage.tile([P, 2, 512, 4], BF16, name="big", bufs=3, align_bytes=64)
+            x_grp.append(big)
         x_codes = [keep.tile([P, 2, 512], U32, name="x_codes%d" % g, align_bytes=64) for g in range(2)]
         x_sc = [keep.tile([P, 2, 512], U8, name="x_sc%d" % g, align_bytes=64) for g in range(2)]
         w_codes = [[keep.tile([P, 512], U32, name="w_codes%d%d" % (h, k), align_bytes=64) for k in range(2)] for h in range(2)]
@@ -76,16 +81,16 @@ def tile_fagcnsignedtanhpropagation_kernel(
         nc.scalar.dma_start(out=xs_col[:], in_=x_scale.rearrange("o (k p t) -> p (o k) t", p=P, t=4))
         nc.scalar.dma_start(out=ri_raw[:], in_=ri.rearrange("(g p t) -> p g t", p=P, t=4))
         nc.scalar.dma_start(out=ro_raw[:], in_=ro.rearrange("(g p t) -> p g t", p=P, t=4))
+        w_in = {}
         for g in range(2):
             for t in (0, 2):
                 nc.sync.dma_start(out=x_in[g][:, t : t + 2, :], in_=x_view[g][:, t : t + 2, :])
             for k in range(2):
-                nc.sync.dma_start(out=w_in[g][k][:], in_=w_view[k][:, :, 512 * g : 512 * g + 512])
+                load = stage.tile([P, 4, 512], BF16, name="load", bufs=4)
+                nc.sync.dma_start(out=load[:], in_=w_view[k][:, :, 512 * g : 512 * g + 512])
+                w_in[g, k] = load
         nc.sync.dma_start(out=a_bc[:, 0, :], in_=a1.partition_broadcast(P))
         nc.sync.dma_start(out=a_bc[:, 1, :], in_=a2.partition_broadcast(P))
-        for g in range(2):
-            for t in (0, 2):
-                nc.sync.dma_start(out=adj_in[g][:, t : t + 2, :], in_=adj_view[g][:, t : t + 2, :])
 
         nc.vector.memset(warm[:], 0.0)
         nc.scalar.activation(out=warm[:], in_=warm[:], func=ACT.Tanh)
@@ -99,27 +104,28 @@ def tile_fagcnsignedtanhpropagation_kernel(
             x_row = stage.tile([P, 1024], BF16, name="x_row", bufs=6)
             if eng == "v":
                 nc.vector.tensor_copy(out=x_row[:], in_=x_in[g][:, t, :].bitcast(FP8))
+            elif eng == "g":
+                nc.gpsimd.tensor_copy(out=x_row[:], in_=x_in[g][:, t, :].bitcast(FP8))
             else:
                 nc.scalar.copy(out=x_row[:], in_=x_in[g][:, t, :].bitcast(FP8))
             x_wide[g, t] = x_row
 
-        def x_turn(g, t):
+        def x_turn(g, p, k):
             ps = psum.tile([P, 2, 2, P], F32, name="turn", bufs=2)
-            words = x_wide[g, t][:].bitcast(F32)
-            for k in range(2):
+            for i in range(2):
+                words = x_wide[g, 2 * p + i][:].bitcast(F32)
                 for u in range(2):
-                    nc.tensor.transpose(ps[:, k, u, :], words[:, 256 * k + u : 256 * (k + 1) : 2], ident[:])
-            x_ps[g, t] = ps
+                    nc.tensor.transpose(ps[:, u, i, :], words[:, 256 * k + u : 256 * (k + 1) : 2], ident[:])
+            x_ps[g, p, k] = ps
 
-        def x_scale_out(g, t):
-            flat = x_ps[g, t][:].rearrange("p k u r -> p (k u r)").bitcast(BF16)
-            for k in range(2):
-                nc.vector.tensor_tensor(
-                    out=x_grp[g][:, k, P * t : P * t + P, :].rearrange("p r (u e) -> p r u e", u=2),
-                    in0=flat[:, 512 * k : 512 * k + 512].rearrange("p (u r e) -> p r u e", u=2, e=2),
-                    in1=xs_col[:, k, :].unsqueeze(1).to_broadcast([P, P, 4]).rearrange("p r (u e) -> p r u e", u=2),
-                    op=MULT,
-                )
+        def x_scale_out(g, p, k):
+            flat = x_ps[g, p, k][:].rearrange("p u i r -> p (u i r)").bitcast(BF16)
+            nc.vector.tensor_tensor(
+                out=x_grp[g][:, k, 2 * P * p : 2 * P * p + 2 * P, :].rearrange("p r (u e) -> p r u e", u=2),
+                in0=flat.rearrange("p (u r e) -> p r u e", u=2, e=2),
+                in1=xs_col[:, k, :].unsqueeze(1).to_broadcast([P, 2 * P, 4]).rearrange("p r (u e) -> p r u e", u=2),
+                op=MULT,
+            )
 
         def x_quant(g, k):
             nc.vector.quantize_mx(
@@ -135,7 +141,7 @@ def tile_fagcnsignedtanhpropagation_kernel(
                 w_grp[h, k] = grp
             lo = 256 * half
             dst = w_grp[h, k][:, lo : lo + 256, :]
-            src = w_in[h][k][:, :, lo : lo + 256].rearrange("p j f -> p f j")
+            src = w_in[h, k][:, :, lo : lo + 256].rearrange("p j f -> p f j")
             if eng == "v":
                 nc.vector.tensor_copy(out=dst, in_=src)
             elif eng == "s":
@@ -173,16 +179,39 @@ def tile_fagcnsignedtanhpropagation_kernel(
 
         def a_cols_out():
             nc.vector.tensor_copy(out=a_col[:], in_=acc_ps["a"][:, :, :, 0])
-            nc.vector.tensor_scalar(out=ri_col[:], in0=ri_raw[:].rearrange("p g t -> p (g t)"), scalar1=1.0 / 0.3, scalar2=None, op0=MULT)
+            nc.vector.tensor_scalar(out=ri_10_3[:], in0=ri_raw[:].rearrange("p g t -> p (g t)"), scalar1=1.0 / 0.3, scalar2=None, op0=MULT)
+            nc.vector.tensor_copy(out=ri_col[:], in_=ri_raw[:].rearrange("p g t -> p (g t)"))
             nc.vector.tensor_copy(out=ro_col[:], in_=ro_raw[:].rearrange("p g t -> p (g t)"))
 
         def zt_out(g, b, eng):
-            sb = stage.tile([P, 512], F32, name="zt_sb%d" % b, bufs=1)
+            sb = stage.tile([P, 512], F32, name="zt_sb%d" % b, bufs=2)
             if eng == "v":
                 nc.vector.tensor_copy(out=sb[:], in_=acc_ps["zt", g, b][:])
             else:
                 nc.scalar.copy(out=sb[:], in_=acc_ps["zt", g, b][:])
             zt_sb[g, b] = sb
+
+        zt_hi = {}
+        zt_lo = {}
+
+        def copy_on(eng, out, in_):
+            if eng == "v":
+                nc.vector.tensor_copy(out=out, in_=in_)
+            elif eng == "s":
+                nc.scalar.copy(out=out, in_=in_)
+            else:
+                nc.gpsimd.tensor_copy(out=out, in_=in_)
+
+        def zt_high(g, b, eng):
+            hi = stage.tile([P, 512], BF16, name="zt_hi%d" % b, bufs=2)
+            copy_on(eng, hi[:], zt_sb[g, b][:])
+            zt_hi[g, b] = hi
+
+        def zt_low(g, b, eng):
+            lo = stage.tile([P, 512], BF16, name="zt_lo%d" % b, bufs=2)
+            e = nc.vector if eng == "v" else nc.gpsimd
+            e.tensor_tensor(out=lo[:], in0=zt_sb[g, b][:], in1=zt_hi[g, b][:], op=SUB)
+            zt_lo[g, b] = lo
 
         st_ps = {}
 
@@ -190,10 +219,11 @@ def tile_fagcnsignedtanhpropagation_kernel(
             ps = psum.tile([P, 4, 2], F32, name="turn", bufs=2)
             for t in range(4):
                 for b in range(NB):
-                    nc.tensor.matmul(
-                        out=ps[:, t, :], lhsT=zt_sb[g, b][:, P * t : P * t + P], rhs=a_col[:, b, :],
-                        start=(b == 0), stop=(b == NB - 1),
-                    )
+                    for q, half in enumerate((zt_hi, zt_lo)):
+                        nc.tensor.matmul(
+                            out=ps[:, t, :], lhsT=half[g, b][:, P * t : P * t + P], rhs=a_col[:, b, :],
+                            start=(b == 0 and q == 0), stop=(b == NB - 1 and q == 1),
+                        )
             st_ps[g] = ps
 
         def z_mm(g, t, h):
@@ -213,12 +243,37 @@ def tile_fagcnsignedtanhpropagation_kernel(
             else:
                 nc.scalar.activation(out=z03[g][h][:, t, :], in_=acc_ps["z", g, t, h][:], func=ACT.Copy, scale=0.3)
 
+        def z_block(g, c):
+            ps = psum.tile([P, 4, P], F32, name="acc", bufs=4)
+            for t in range(4):
+                nc.tensor.transpose(ps[:, t, :], zt_sb[g, c][:, P * t : P * t + P], ident[:])
+            acc_ps["zd", g, c] = ps
+
+        def z_block_out(g, c, eng):
+            dst = z03[g][0][:, :, P * c : P * c + P]
+            if eng == "v":
+                nc.vector.tensor_scalar(out=dst, in0=acc_ps["zd", g, c][:], scalar1=0.3, scalar2=None, op0=MULT)
+            else:
+                nc.scalar.activation(out=dst, in_=acc_ps["zd", g, c][:], func=ACT.Copy, scale=0.3)
+
+        product = {}
+
+        def z_product(g, t, h, a):
+            prod = stage.tile([P, 512], F32, name="prod", bufs=2)
+            nc.gpsimd.tensor_tensor(out=prod[:], in0=z03[g][h][:, t, :], in1=a_bc[:, a, 512 * h : 512 * h + 512], op=MULT)
+            product[g, t, a] = prod
+
         def z_score(g, t, h, a):
-            junk = stage.tile([P, 512], BF16, name="junk", bufs=2)
-            nc.vector.scalar_tensor_tensor(
-                out=junk[:], in0=acc_ps["z", g, t, h][:], scalar=1.0, in1=a_bc[:, a, 512 * h : 512 * h + 512],
-                op0=MULT, op1=MULT, accum_out=part[g][:, a, t : t + 1],
-            )
+            into = part[g][:, a, t : t + 1]
+            if (g, t, a) in product:
+                junk_s = stage.tile([P, 512], BF16, name="junk_s", bufs=2)
+                nc.scalar.activation(out=junk_s[:], in_=product[g, t, a][:], func=ACT.Copy, scale=1.0 / 0.3, accum_out=into)
+            else:
+                junk = stage.tile([P, 512], BF16, name="junk", bufs=2)
+                nc.vector.scalar_tensor_tensor(
+                    out=junk[:], in0=acc_ps["z", g, t, h][:], scalar=1.0, in1=a_bc[:, a, 512 * h : 512 * h + 512],
+                    op0=MULT, op1=MULT, accum_out=into,
+                )
 
         def score_sum(g):
             nc.vector.tensor_tensor(out=score[g][:], in0=st_ps[g][:].rearrange("p t a -> p a t"), in1=part[g][:], op=ADD)
@@ -234,29 +289,66 @@ def tile_fagcnsignedtanhpropagation_kernel(
         gate = {}
 
         def gate_tanh(j, v):
-            tile = stage.tile([P, 4, 2 * P], F32, name="gate", bufs=6)
             g, lo = v // 2, 2 * P * (v % 2)
+            if (j, g) not in gate:
+                big = stage.tile([P, 4, 4 * P], F32, name="big", bufs=3, align_bytes=64)
+                gate[j, g] = big
             for t in range(4):
-                nc.scalar.activation(out=tile[:, t, :], in_=s_row[g][:, lo : lo + 2 * P], func=ACT.Tanh, bias=score[j][:, 1, t : t + 1])
-            gate[j, v] = tile
+                nc.scalar.activation(
+                    out=gate[j, g][:, t, lo : lo + 2 * P], in_=s_row[g][:, lo : lo + 2 * P], func=ACT.Tanh, bias=score[j][:, 1, t : t + 1],
+                )
 
+        zs_row = {}
         zs_grp = {}
 
-        def zs_mul(g, h, c):
+        def zs_scale(g, t, h, eng):
+            if (g, h) not in zs_row:
+                row = stage.tile([P, 4, 512], BF16, name="zs_row", bufs=2)
+                zs_row[g, h] = row
+            dst, src, col = zs_row[g, h][:, t, :], z03[g][h][:, t, :], ri_10_3[:, 4 * g + t : 4 * g + t + 1]
+            if eng == "v":
+                nc.vector.tensor_scalar(out=dst, in0=src, scalar1=col, scalar2=None, op0=MULT)
+            else:
+                nc.scalar.activation(out=dst, in_=src, func=ACT.Copy, scale=col)
+
+        def zs_mix(g, h, c, eng="v"):
             if (g, h) not in zs_grp:
                 grp = stage.tile([P, 512, 4], BF16, name="grp", bufs=4, align_bytes=64)
                 zs_grp[g, h] = grp
             lo = P * c
-            nc.gpsimd.tensor_tensor(
-                out=zs_grp[g, h][:, lo : lo + P, :], in0=z03[g][h][:, :, lo : lo + P].rearrange("p t f -> p f t"),
-                in1=ri_col[:, 4 * g : 4 * g + 4].unsqueeze(1).to_broadcast([P, P, 4]), op=MULT,
-            )
+            dst = zs_grp[g, h][:, lo : lo + P, :]
+            if (g, h) in zs_row:
+                src = zs_row[g, h][:, :, lo : lo + P].rearrange("p t f -> p f t")
+                if eng == "v":
+                    nc.vector.tensor_copy(out=dst, in_=src)
+                else:
+                    nc.gpsimd.tensor_scalar(out=dst, in0=src, scalar1=1.0, scalar2=0.0, op0=MULT, op1=ADD)
+            elif ("zd", g, c) in acc_ps and h == 0:
+                nc.vector.tensor_tensor(
+                    out=dst, in0=acc_ps["zd", g, c][:].rearrange("p t f -> p f t"),
+                    in1=ri_col[:, 4 * g : 4 * g + 4].unsqueeze(1).to_broadcast([P, P, 4]), op=MULT,
+                )
+            else:
+                e = nc.vector if eng == "v" else nc.gpsimd
+                e.tensor_tensor(
+                    out=dst, in0=z03[g][h][:, :, lo : lo + P].rearrange("p t f -> p f t"),
+                    in1=ri_10_3[:, 4 * g : 4 * g + 4].unsqueeze(1).to_broadcast([P, P, 4]), op=MULT,
+                )
 
         def zs_quant(g, h):
             nc.vector.quantize_mx(
                 out=zs_codes[g][h][:].bitcast(FP8X4), scales=zs_sc[g][h][:],
                 in_=zs_grp[g, h][:].rearrange("p n j -> p (n j)"),
             )
+
+        adj_in = {}
+
+        def adj_load():
+            for g in range(2):
+                for q in range(2):
+                    load = stage.tile([P, 2, 1024], BF16, name="load", bufs=4)
+                    nc.sync.dma_start(out=load[:], in_=adj_view[g][:, 2 * q : 2 * q + 2, :])
+                    adj_in[g, q] = load
 
         adj_ps = {}
         c_grp = {}
@@ -265,27 +357,27 @@ def tile_fagcnsignedtanhpropagation_kernel(
             ps = psum.tile([P, 2, 2, P], F32, name="turn", bufs=2)
             for i in range(2):
                 g, t = divmod(2 * v + i, 4)
-                words = adj_in[g][:, t, :].bitcast(F32)
+                words = adj_in[g, t // 2][:, t % 2, :].bitcast(F32)
                 for u in range(2):
-                    nc.tensor.transpose(ps[:, i, u, :], words[:, 256 * j + u : 256 * (j + 1) : 2], ident[:])
+                    nc.tensor.transpose(ps[:, u, i, :], words[:, 256 * j + u : 256 * (j + 1) : 2], ident[:])
             adj_ps[j, v] = ps
 
-        def c_mul(j, v, i):
-            if (j, v) not in c_grp:
-                grp = stage.tile([P, 2, P, 4], BF16, name="c_grp", bufs=6, align_bytes=64)
-                c_grp[j, v] = grp
-            flat = adj_ps[j, v][:].rearrange("p i u r -> p (i u r)").bitcast(BF16)
+        def c_mul(j, v):
+            grp = stage.tile([P, 2 * P, 4], BF16, name="c_grp", bufs=6, align_bytes=64)
+            flat = adj_ps[j, v][:].rearrange("p u i r -> p (u i r)").bitcast(BF16)
+            lo = 2 * P * (v % 2)
             nc.vector.tensor_tensor(
-                out=c_grp[j, v][:, i, :, :].rearrange("p r (u e) -> p r u e", u=2),
-                in0=flat[:, 512 * i : 512 * i + 512].rearrange("p (u r e) -> p r u e", u=2, e=2),
-                in1=gate[j, v][:, :, P * i : P * i + P].rearrange("p (u e) r -> p r u e", u=2),
+                out=grp[:].rearrange("p r (u e) -> p r u e", u=2),
+                in0=flat.rearrange("p (u r e) -> p r u e", u=2, e=2),
+                in1=gate[j, v // 2][:, :, lo : lo + 2 * P].rearrange("p (u e) r -> p r u e", u=2),
                 op=MULT,
             )
+            c_grp[j, v] = grp
 
         def c_quant(j, v):
             nc.vector.quantize_mx(
                 out=c_codes[j][v][:].bitcast(FP8X4), scales=c_sc[j][v][:],
-                in_=c_grp[j, v][:].rearrange("p i r j -> p (i r j)"),
+                in_=c_grp[j, v][:].rearrange("p r j -> p (r j)"),
             )
 
         def m_mm(n, h):
@@ -327,8 +419,8 @@ def tile_fagcnsignedtanhpropagation_kernel(
 
         steps = {
             "xc": x_widen, "xt": x_turn, "xm": x_scale_out, "xq": x_quant, "wm": w_mix, "wq": w_quant,
-            "ac": a_cols, "ao": a_cols_out, "zt": zt_mm, "zo": z_out, "zs": z_score, "sm": score_mm, "ss": score_sum, "sp": s_spread,
-            "th": gate_tanh, "zm": zs_mul, "zq": zs_quant, "at": adj_turn, "cm": c_mul, "cq": c_quant,
+            "la": adj_load, "ac": a_cols, "ao": a_cols_out, "zt": zt_mm, "zo": z_out, "zs": z_score, "sm": score_mm, "ss": score_sum, "sp": s_spread,
+            "th": gate_tanh, "zm": zs_mix, "zr": zs_scale, "tz": z_block, "hi": zt_high, "lo": zt_low, "zp": z_block_out, "pg": z_product, "zq": zs_quant, "at": adj_turn, "cm": c_mul, "cq": c_quant,
             "f": finish, "fs": m_out, "fg": finish_add, "m": m_mm, "z": z_mm, "zto": zt_out,
         }
         for token in ORDER.split():

from contextlib import ExitStack

import concourse.mybir as mybir
from concourse.masks import make_identity

F32 = mybir.dt.float32
BF16 = mybir.dt.bfloat16
U32 = mybir.dt.uint32
U8 = mybir.dt.uint8
FP8 = mybir.dt.float8_e4m3fn
FP8X4 = mybir.dt.float8_e4m3fn_x4
MULT = mybir.AluOpType.mult
ADD = mybir.AluOpType.add
SUB = mybir.AluOpType.subtract
ACT = mybir.ActivationFunctionType

NODES, FEATS = 1024, 1024
P = 128
FLOPS = 2 * 2 * NODES * FEATS * 1024
ORDER = """
    xc00v xc01s xc02v xc03v xt001 wm001s wm000g xt011 xm001 wm010s wm011g xm011 xt000 xc12s xq01
    xt010 xc10s wq00 xm000 wm111g xc11s xm010 xc13s xt101 wq01 wm101s xt100 xq00 xm101 wm100s zt03
    xm100 wm110s la xt110 zt02 wq10 zto03s zt00 xm110 zto02s ac hi03s wq11 zto00s xt111 xq10 hi02s
    zt01 lo03g xm111 z011 zto01s zo011s xq11 hi00s lo02g zs0110 zt13 hi01s aco zt11 zs0111 lo00g z001
    zto13v zto11s z021 zs0011 hi13s zt12 hi11g zo001s zs0211 z031 lo01g zo021s zs0010 zo031s zs0210
    zt10 lo13g zto12s zs0310 z111 zr001s zs0311 z101 zr021s hi12g zs1111 z121 zr031s lo11g zs1010
    zto10s zs1211 zr011s z131 zs1110 zo101s zm012g sm0 zo121s zs1311 lo12g zo111s zs1011 zo131s
    zs1210 tz01 zm013g hi10s tz02 ss0 zs1310 zr111s sp0 lo10g zm001 tz10 zr131s tz11 zm002 th00 at00
    zm010g zm100 sm1 zm101 zm011g zp01s cm00 zp02s tz13 zr121s tz12 zq01 zr101s at01 cq00 th01 ss1
    zm111g zm103 at10 zm102 zm110g sp1 th10 cm01 zm113g th02 cm10 zm112g at02 zp10s zq10 at12 zp11s
    cq10 zq11 th12 cq01 m11 cm02 th11 cm12 at11 zp13s tz00 zp12s cq02 m01 cq12 fs11 cm11 tz03 zp00s
    fg11 at03 th03 zm000 at13 zm003 m41 fs01 cq11 zq00 zp03s m21 cm03 fg01 fs41 m30 fs21 m10 f30 fg41
    th13 m20 f10 m31 f20 m51 fg21 fs31 cm13 m40 fs51 m00 cq03 m50 cq13 f40 fg51 m71 f00 m61 f50 fg31
    m60 f61 m70 f71 f60 f70
"""
NB = 4


def tile_fagcnsignedtanhpropagation_kernel(
    tc, x_bytes, x_scale, w, adj, a1, a2, ri, ro, out
):
    nc = tc.nc
    with ExitStack() as ctx:
        keep = ctx.enter_context(tc.tile_pool(name="keep", bufs=1))
        stage = ctx.enter_context(tc.tile_pool(name="stage", bufs=2))
        psum = ctx.enter_context(tc.psum_pool(name="psum", bufs=1))
        ctx.enter_context(tc.manual_schedule())

        xs_col = keep.tile([P, 2, 4], F32, name="xs_col")
        a_bc = keep.tile([P, 2, 1024], BF16, name="a_bc")
        ri_raw = keep.tile([P, 2, 4], BF16, name="ri_raw")
        ro_raw = keep.tile([P, 2, 4], BF16, name="ro_raw")
        ri_col = keep.tile([P, 8], F32, name="ri_col")
        ri_10_3 = keep.tile([P, 8], F32, name="ri_10_3")
        ro_col = keep.tile([P, 8], F32, name="ro_col")
        ident = keep.tile([P, P], F32, name="ident")
        ident_bf = keep.tile([P, P], BF16, name="ident_bf")
        a_col = keep.tile([P, NB, 2], BF16, name="a_col")
        warm = keep.tile([P, 1], F32, name="warm")
        x_in = [keep.tile([P, 4, 1024], U8, name="x_in%d" % g) for g in range(2)]
        x_grp = []
        for g in range(2):
            big = stage.tile([P, 2, 512, 4], BF16, name="big", bufs=3, align_bytes=64)
            x_grp.append(big)
        x_codes = [keep.tile([P, 2, 512], U32, name="x_codes%d" % g, align_bytes=64) for g in range(2)]
        x_sc = [keep.tile([P, 2, 512], U8, name="x_sc%d" % g, align_bytes=64) for g in range(2)]
        w_codes = [[keep.tile([P, 512], U32, name="w_codes%d%d" % (h, k), align_bytes=64) for k in range(2)] for h in range(2)]
        w_sc = [[keep.tile([P, 512], U8, name="w_sc%d%d" % (h, k), align_bytes=64) for k in range(2)] for h in range(2)]
        z03 = [[keep.tile([P, 4, 512], F32, name="z03_%d%d" % (g, h)) for h in range(2)] for g in range(2)]
        zs_codes = [[keep.tile([P, 512], U32, name="zs_codes%d%d" % (g, h), align_bytes=64) for h in range(2)] for g in range(2)]
        zs_sc = [[keep.tile([P, 512], U8, name="zs_sc%d%d" % (g, h), align_bytes=64) for h in range(2)] for g in range(2)]
        c_codes = [[keep.tile([P, 256], U32, name="c_codes%d%d" % (j, u), align_bytes=64) for u in range(4)] for j in range(2)]
        c_sc = [[keep.tile([P, 256], U8, name="c_sc%d%d" % (j, u), align_bytes=64) for u in range(4)] for j in range(2)]
        part = [keep.tile([P, 2, 4], F32, name="part%d" % g) for g in range(2)]
        score = [keep.tile([P, 2, 4], F32, name="score%d" % g) for g in range(2)]

        x_view = x_bytes.rearrange("(g p t) k -> g p t k", p=P, t=4)
        w_view = w.rearrange("(k p j) f -> k p j f", p=P, j=4)
        adj_view = adj.rearrange("(g p t) j -> g p t j", p=P, t=4)
        out_view = out.rearrange("(g p t) f -> g t p f", p=P, t=4)
        nc.scalar.dma_start(out=xs_col[:], in_=x_scale.rearrange("o (k p t) -> p (o k) t", p=P, t=4))
        nc.scalar.dma_start(out=ri_raw[:], in_=ri.rearrange("(g p t) -> p g t", p=P, t=4))
        nc.scalar.dma_start(out=ro_raw[:], in_=ro.rearrange("(g p t) -> p g t", p=P, t=4))
        w_in = {}
        for g in range(2):
            for t in (0, 2):
                nc.sync.dma_start(out=x_in[g][:, t : t + 2, :], in_=x_view[g][:, t : t + 2, :])
            for k in range(2):
                load = stage.tile([P, 4, 512], BF16, name="load", bufs=4)
                nc.sync.dma_start(out=load[:], in_=w_view[k][:, :, 512 * g : 512 * g + 512])
                w_in[g, k] = load
        nc.sync.dma_start(out=a_bc[:, 0, :], in_=a1.partition_broadcast(P))
        nc.sync.dma_start(out=a_bc[:, 1, :], in_=a2.partition_broadcast(P))

        nc.vector.memset(warm[:], 0.0)
        nc.scalar.activation(out=warm[:], in_=warm[:], func=ACT.Tanh)
        make_identity(nc, ident[:])
        make_identity(nc, ident_bf[:])

        x_wide = {}
        x_ps = {}

        def x_widen(g, t, eng):
            x_row = stage.tile([P, 1024], BF16, name="x_row", bufs=6)
            if eng == "v":
                nc.vector.tensor_copy(out=x_row[:], in_=x_in[g][:, t, :].bitcast(FP8))
            elif eng == "g":
                nc.gpsimd.tensor_copy(out=x_row[:], in_=x_in[g][:, t, :].bitcast(FP8))
            else:
                nc.scalar.copy(out=x_row[:], in_=x_in[g][:, t, :].bitcast(FP8))
            x_wide[g, t] = x_row

        def x_turn(g, p, k):
            ps = psum.tile([P, 2, 2, P], F32, name="turn", bufs=2)
            for i in range(2):
                words = x_wide[g, 2 * p + i][:].bitcast(F32)
                for u in range(2):
                    nc.tensor.transpose(ps[:, u, i, :], words[:, 256 * k + u : 256 * (k + 1) : 2], ident[:])
            x_ps[g, p, k] = ps

        def x_scale_out(g, p, k):
            flat = x_ps[g, p, k][:].rearrange("p u i r -> p (u i r)").bitcast(BF16)
            nc.vector.tensor_tensor(
                out=x_grp[g][:, k, 2 * P * p : 2 * P * p + 2 * P, :].rearrange("p r (u e) -> p r u e", u=2),
                in0=flat.rearrange("p (u r e) -> p r u e", u=2, e=2),
                in1=xs_col[:, k, :].unsqueeze(1).to_broadcast([P, 2 * P, 4]).rearrange("p r (u e) -> p r u e", u=2),
                op=MULT,
            )

        def x_quant(g, k):
            nc.vector.quantize_mx(
                out=x_codes[g][:, k, :].bitcast(FP8X4), scales=x_sc[g][:, k, :],
                in_=x_grp[g][:, k, :, :].rearrange("p n j -> p (n j)"),
            )

        w_grp = {}

        def w_mix(h, k, half, eng):
            if (h, k) not in w_grp:
                grp = stage.tile([P, 512, 4], BF16, name="grp", bufs=4, align_bytes=64)
                w_grp[h, k] = grp
            lo = 256 * half
            dst = w_grp[h, k][:, lo : lo + 256, :]
            src = w_in[h, k][:, :, lo : lo + 256].rearrange("p j f -> p f j")
            if eng == "v":
                nc.vector.tensor_copy(out=dst, in_=src)
            elif eng == "s":
                nc.scalar.copy(out=dst, in_=src)
            else:
                nc.gpsimd.tensor_scalar(out=dst, in0=src, scalar1=1.0, scalar2=0.0, op0=MULT, op1=ADD)

        def w_quant(h, k):
            nc.vector.quantize_mx(
                out=w_codes[h][k][:].bitcast(FP8X4), scales=w_sc[h][k][:],
                in_=w_grp[h, k][:].rearrange("p n j -> p (n j)"),
            )

        zt_sb = {}
        acc_ps = {}

        def zt_mm(g, b):
            h, c = divmod(b, 4)
            ps = psum.tile([P, 512], F32, name="acc", bufs=4)
            for k in range(2):
                nc.tensor.matmul_mx(
                    out=ps[:],
                    lhsT=w_codes[h][k][:, P * c : P * c + P].bitcast(FP8X4), lhsT_scale=w_sc[h][k][:, P * c : P * c + P],
                    rhs=x_codes[g][:, k, :].bitcast(FP8X4), rhs_scale=x_sc[g][:, k, :],
                    start=(k == 0), stop=(k == 1),
                )
            acc_ps["zt", g, b] = ps

        def a_cols():
            ps = psum.tile([P, NB, 2, P], BF16, name="turn", bufs=2)
            for b in range(NB):
                for a in range(2):
                    nc.tensor.transpose(ps[:, b, a, :], a_bc[:, a, P * b : P * b + P], ident_bf[:])
            acc_ps["a"] = ps

        def a_cols_out():
            nc.vector.tensor_copy(out=a_col[:], in_=acc_ps["a"][:, :, :, 0])
            nc.vector.tensor_scalar(out=ri_10_3[:], in0=ri_raw[:].rearrange("p g t -> p (g t)"), scalar1=1.0 / 0.3, scalar2=None, op0=MULT)
            nc.vector.tensor_copy(out=ri_col[:], in_=ri_raw[:].rearrange("p g t -> p (g t)"))
            nc.vector.tensor_copy(out=ro_col[:], in_=ro_raw[:].rearrange("p g t -> p (g t)"))

        def zt_out(g, b, eng):
            sb = stage.tile([P, 512], F32, name="zt_sb%d" % b, bufs=2)
            if eng == "v":
                nc.vector.tensor_copy(out=sb[:], in_=acc_ps["zt", g, b][:])
            else:
                nc.scalar.copy(out=sb[:], in_=acc_ps["zt", g, b][:])
            zt_sb[g, b] = sb

        zt_hi = {}
        zt_lo = {}

        def copy_on(eng, out, in_):
            if eng == "v":
                nc.vector.tensor_copy(out=out, in_=in_)
            elif eng == "s":
                nc.scalar.copy(out=out, in_=in_)
            else:
                nc.gpsimd.tensor_copy(out=out, in_=in_)

        def zt_high(g, b, eng):
            hi = stage.tile([P, 512], BF16, name="zt_hi%d" % b, bufs=2)
            copy_on(eng, hi[:], zt_sb[g, b][:])
            zt_hi[g, b] = hi

        def zt_low(g, b, eng):
            lo = stage.tile([P, 512], BF16, name="zt_lo%d" % b, bufs=2)
            e = nc.vector if eng == "v" else nc.gpsimd
            e.tensor_tensor(out=lo[:], in0=zt_sb[g, b][:], in1=zt_hi[g, b][:], op=SUB)
            zt_lo[g, b] = lo

        st_ps = {}

        def score_mm(g):
            ps = psum.tile([P, 4, 2], F32, name="turn", bufs=2)
            for t in range(4):
                for b in range(NB):
                    for q, half in enumerate((zt_hi, zt_lo)):
                        nc.tensor.matmul(
                            out=ps[:, t, :], lhsT=half[g, b][:, P * t : P * t + P], rhs=a_col[:, b, :],
                            start=(b == 0 and q == 0), stop=(b == NB - 1 and q == 1),
                        )
            st_ps[g] = ps

        def z_mm(g, t, h):
            ps = psum.tile([P, 512], F32, name="acc", bufs=4)
            for k in range(2):
                nc.tensor.matmul_mx(
                    out=ps[:],
                    lhsT=x_codes[g][:, k, P * t : P * t + P].bitcast(FP8X4), lhsT_scale=x_sc[g][:, k, P * t : P * t + P],
                    rhs=w_codes[h][k][:].bitcast(FP8X4), rhs_scale=w_sc[h][k][:],
                    start=(k == 0), stop=(k == 1),
                )
            acc_ps["z", g, t, h] = ps

        def z_out(g, t, h, eng):
            if eng == "v":
                nc.vector.tensor_scalar(out=z03[g][h][:, t, :], in0=acc_ps["z", g, t, h][:], scalar1=0.3, scalar2=None, op0=MULT)
            else:
                nc.scalar.activation(out=z03[g][h][:, t, :], in_=acc_ps["z", g, t, h][:], func=ACT.Copy, scale=0.3)

        def z_block(g, c):
            ps = psum.tile([P, 4, P], F32, name="acc", bufs=4)
            for t in range(4):
                nc.tensor.transpose(ps[:, t, :], zt_sb[g, c][:, P * t : P * t + P], ident[:])
            acc_ps["zd", g, c] = ps

        def z_block_out(g, c, eng):
            dst = z03[g][0][:, :, P * c : P * c + P]
            if eng == "v":
                nc.vector.tensor_scalar(out=dst, in0=acc_ps["zd", g, c][:], scalar1=0.3, scalar2=None, op0=MULT)
            else:
                nc.scalar.activation(out=dst, in_=acc_ps["zd", g, c][:], func=ACT.Copy, scale=0.3)

        product = {}

        def z_product(g, t, h, a):
            prod = stage.tile([P, 512], F32, name="prod", bufs=2)
            nc.gpsimd.tensor_tensor(out=prod[:], in0=z03[g][h][:, t, :], in1=a_bc[:, a, 512 * h : 512 * h + 512], op=MULT)
            product[g, t, a] = prod

        def z_score(g, t, h, a):
            into = part[g][:, a, t : t + 1]
            if (g, t, a) in product:
                junk_s = stage.tile([P, 512], BF16, name="junk_s", bufs=2)
                nc.scalar.activation(out=junk_s[:], in_=product[g, t, a][:], func=ACT.Copy, scale=1.0 / 0.3, accum_out=into)
            else:
                junk = stage.tile([P, 512], BF16, name="junk", bufs=2)
                nc.vector.scalar_tensor_tensor(
                    out=junk[:], in0=acc_ps["z", g, t, h][:], scalar=1.0, in1=a_bc[:, a, 512 * h : 512 * h + 512],
                    op0=MULT, op1=MULT, accum_out=into,
                )

        def score_sum(g):
            nc.vector.tensor_tensor(out=score[g][:], in0=st_ps[g][:].rearrange("p t a -> p a t"), in1=part[g][:], op=ADD)

        s_row = {}

        def s_spread(g):
            ps = psum.tile([P, 512], F32, name="srow%d" % g, bufs=1)
            for t in range(4):
                nc.tensor.transpose(ps[:, P * t : P * t + P], score[g][:, 0, t : t + 1].to_broadcast([P, P]), ident[:])
            s_row[g] = ps

        gate = {}

        def gate_tanh(j, v):
            g, lo = v // 2, 2 * P * (v % 2)
            if (j, g) not in gate:
                big = stage.tile([P, 4, 4 * P], F32, name="big", bufs=3, align_bytes=64)
                gate[j, g] = big
            for t in range(4):
                nc.scalar.activation(
                    out=gate[j, g][:, t, lo : lo + 2 * P], in_=s_row[g][:, lo : lo + 2 * P], func=ACT.Tanh, bias=score[j][:, 1, t : t + 1],
                )

        zs_row = {}
        zs_grp = {}

        def zs_scale(g, t, h, eng):
            if (g, h) not in zs_row:
                row = stage.tile([P, 4, 512], BF16, name="zs_row", bufs=2)
                zs_row[g, h] = row
            dst, src, col = zs_row[g, h][:, t, :], z03[g][h][:, t, :], ri_10_3[:, 4 * g + t : 4 * g + t + 1]
            if eng == "v":
                nc.vector.tensor_scalar(out=dst, in0=src, scalar1=col, scalar2=None, op0=MULT)
            else:
                nc.scalar.activation(out=dst, in_=src, func=ACT.Copy, scale=col)

        def zs_mix(g, h, c, eng="v"):
            if (g, h) not in zs_grp:
                grp = stage.tile([P, 512, 4], BF16, name="grp", bufs=4, align_bytes=64)
                zs_grp[g, h] = grp
            lo = P * c
            dst = zs_grp[g, h][:, lo : lo + P, :]
            if (g, h) in zs_row:
                src = zs_row[g, h][:, :, lo : lo + P].rearrange("p t f -> p f t")
                if eng == "v":
                    nc.vector.tensor_copy(out=dst, in_=src)
                else:
                    nc.gpsimd.tensor_scalar(out=dst, in0=src, scalar1=1.0, scalar2=0.0, op0=MULT, op1=ADD)
            elif ("zd", g, c) in acc_ps and h == 0:
                nc.vector.tensor_tensor(
                    out=dst, in0=acc_ps["zd", g, c][:].rearrange("p t f -> p f t"),
                    in1=ri_col[:, 4 * g : 4 * g + 4].unsqueeze(1).to_broadcast([P, P, 4]), op=MULT,
                )
            else:
                e = nc.vector if eng == "v" else nc.gpsimd
                e.tensor_tensor(
                    out=dst, in0=z03[g][h][:, :, lo : lo + P].rearrange("p t f -> p f t"),
                    in1=ri_10_3[:, 4 * g : 4 * g + 4].unsqueeze(1).to_broadcast([P, P, 4]), op=MULT,
                )

        def zs_quant(g, h):
            nc.vector.quantize_mx(
                out=zs_codes[g][h][:].bitcast(FP8X4), scales=zs_sc[g][h][:],
                in_=zs_grp[g, h][:].rearrange("p n j -> p (n j)"),
            )

        adj_in = {}

        def adj_load():
            for g in range(2):
                for q in range(2):
                    load = stage.tile([P, 2, 1024], BF16, name="load", bufs=4)
                    nc.sync.dma_start(out=load[:], in_=adj_view[g][:, 2 * q : 2 * q + 2, :])
                    adj_in[g, q] = load

        adj_ps = {}
        c_grp = {}

        def adj_turn(j, v):
            ps = psum.tile([P, 2, 2, P], F32, name="turn", bufs=2)
            for i in range(2):
                g, t = divmod(2 * v + i, 4)
                words = adj_in[g, t // 2][:, t % 2, :].bitcast(F32)
                for u in range(2):
                    nc.tensor.transpose(ps[:, u, i, :], words[:, 256 * j + u : 256 * (j + 1) : 2], ident[:])
            adj_ps[j, v] = ps

        def c_mul(j, v):
            grp = stage.tile([P, 2 * P, 4], BF16, name="c_grp", bufs=6, align_bytes=64)
            flat = adj_ps[j, v][:].rearrange("p u i r -> p (u i r)").bitcast(BF16)
            lo = 2 * P * (v % 2)
            nc.vector.tensor_tensor(
                out=grp[:].rearrange("p r (u e) -> p r u e", u=2),
                in0=flat.rearrange("p (u r e) -> p r u e", u=2, e=2),
                in1=gate[j, v // 2][:, :, lo : lo + 2 * P].rearrange("p (u e) r -> p r u e", u=2),
                op=MULT,
            )
            c_grp[j, v] = grp

        def c_quant(j, v):
            nc.vector.quantize_mx(
                out=c_codes[j][v][:].bitcast(FP8X4), scales=c_sc[j][v][:],
                in_=c_grp[j, v][:].rearrange("p r j -> p (r j)"),
            )

        def m_mm(n, h):
            v, i = divmod(n, 2)
            ps = psum.tile([P, 512], F32, name="acc", bufs=4)
            for j in range(2):
                nc.tensor.matmul_mx(
                    out=ps[:],
                    lhsT=c_codes[j][v][:, P * i : P * i + P].bitcast(FP8X4), lhsT_scale=c_sc[j][v][:, P * i : P * i + P],
                    rhs=zs_codes[j][h][:].bitcast(FP8X4), rhs_scale=zs_sc[j][h][:],
                    start=(j == 0), stop=(j == 1),
                )
            acc_ps["m", n, h] = ps

        def store(n, h, res):
            g, t = divmod(n, 4)
            nc.sync.dma_start(out=out_view[g][t][:, 512 * h : 512 * h + 512], in_=res[:])

        def finish(n, h):
            g, t = divmod(n, 4)
            res = stage.tile([P, 512], F32, name="res", bufs=4)
            nc.vector.scalar_tensor_tensor(
                out=res[:], in0=acc_ps["m", n, h][:], scalar=ro_col[:, n : n + 1], in1=z03[g][h][:, t, :], op0=MULT, op1=ADD,
            )
            store(n, h, res)

        m_scaled = {}

        def m_out(n, h):
            mro = stage.tile([P, 512], F32, name="mro", bufs=3)
            nc.scalar.activation(out=mro[:], in_=acc_ps["m", n, h][:], func=ACT.Copy, scale=ro_col[:, n : n + 1])
            m_scaled[n, h] = mro

        def finish_add(n, h):
            g, t = divmod(n, 4)
            res = stage.tile([P, 512], F32, name="res_g", bufs=2)
            nc.gpsimd.tensor_tensor(out=res[:], in0=m_scaled[n, h][:], in1=z03[g][h][:, t, :], op=ADD)
            store(n, h, res)

        steps = {
            "xc": x_widen, "xt": x_turn, "xm": x_scale_out, "xq": x_quant, "wm": w_mix, "wq": w_quant,
            "la": adj_load, "ac": a_cols, "ao": a_cols_out, "zt": zt_mm, "zo": z_out, "zs": z_score, "sm": score_mm, "ss": score_sum, "sp": s_spread,
            "th": gate_tanh, "zm": zs_mix, "zr": zs_scale, "tz": z_block, "hi": zt_high, "lo": zt_low, "zp": z_block_out, "pg": z_product, "zq": zs_quant, "at": adj_turn, "cm": c_mul, "cq": c_quant,
            "f": finish, "fs": m_out, "fg": finish_add, "m": m_mm, "z": z_mm, "zto": zt_out,
        }
        for token in ORDER.split():
            word = token.replace("aco", "ao")
            name = "".join([ch for ch in word if ch not in "0123456789"])
            args = [int(ch) for ch in word if ch in "0123456789"]
            eng = []
            if name not in steps:
                eng = [name[-1:]]
                name = name[:-1]
            if name == "th":
                args = args[:2]
            steps[name](*args, *eng)
